import numpy as np
import ml_dtypes


def mxq(x, axis, fmt="e4m3"):
    dtype, down = {"e4m3": (ml_dtypes.float8_e4m3fn, 7), "e5m2": (ml_dtypes.float8_e5m2, 14)}[fmt]
    v = np.moveaxis(np.asarray(x, np.float32).astype(ml_dtypes.bfloat16).astype(np.float64), axis, -1)
    blocks = v.reshape(v.shape[:-1] + (-1, 32))
    amax = np.abs(blocks).max(-1, keepdims=True)
    byte = np.maximum(np.where(amax > 0, np.frexp(amax)[1] - 1 + 127, 0) - down, 1)
    scale = np.exp2(byte - 127.0)
    codes = (blocks / scale).astype(np.float32).astype(dtype).astype(np.float64)
    return np.moveaxis((codes * scale).reshape(v.shape), -1, axis)


WIDE = False


def mx_kscale(k):
    if not WIDE:
        return np.ones(k)
    levels = np.array([10, -10, 5, -5, 0])
    if k % 512:
        return np.exp2(np.random.permutation(np.resize(levels, k // 32))).repeat(32)
    a = np.empty((k // 512, 16))
    for p in range(k // 512):
        a[p, :8] = np.random.permutation(np.resize(levels, 8))
        for g in range(8):
            far = levels[np.abs(levels - a[p, g]) >= 10]
            a[p, g + 8] = far[np.random.randint(len(far))]
    return np.exp2(a.ravel()).repeat(32)


def f64(x):
    return np.asarray(x).astype(np.float64)


def striped(idx):
    return np.tile(np.asarray(idx).reshape(-1, 16).T, (8, 1)).astype(np.uint16)


def unstriped(offs):
    return offs[:16].T.reshape(-1).astype(np.int64)


def striped8(idx):
    return np.asarray(idx).reshape(8, -1, 16).transpose(0, 2, 1).reshape(128, -1).astype(np.uint16)


def unstriped8(offs):
    return offs.reshape(8, 16, -1).transpose(0, 2, 1).reshape(8, -1).astype(np.int64)


def pick8(x, idx, run):
    r = np.arange(len(x))
    return x[r[:, None], idx[r % (8 * run) // run]]


E2M1 = np.array([0.0, 0.5, 1.0, 1.5, 2.0, 3.0, 4.0, 6.0, -0.0, -0.5, -1.0, -1.5, -2.0, -3.0, -4.0, -6.0])


def pack_weight(w, fmt):
    k, n = w.shape
    w = f64(np.asarray(w, np.float32).astype(ml_dtypes.bfloat16)).reshape(k // 32, 32, n)
    amax = np.abs(w).max(1)
    if fmt == "e4m3":
        byte = np.frexp(amax)[1] - 1 + 127 - 7
    else:
        mant, ex = np.frexp(amax / 6.0)
        byte = np.where(mant > 0.5, ex, ex - 1) + 127
    byte = np.clip(np.where(amax > 0, byte, 1), 1, 254)
    scaled = (w * np.exp2(127.0 - byte)[:, None, :]).reshape(k, n).astype(np.float32)
    by_word = np.ascontiguousarray(scaled.reshape(k // 512, 128, 4, n).transpose(0, 1, 3, 2))
    if fmt == "e4m3":
        words = by_word.astype(ml_dtypes.float8_e4m3fn).view(np.uint8)
    else:
        c = by_word.astype(ml_dtypes.float4_e2m1fn).view(np.uint8) & 0xF
        words = (c[..., 0::2] | (c[..., 1::2] << 4)).reshape(k // 512, 128, 2 * n)
    return np.ascontiguousarray(words), np.ascontiguousarray(byte.astype(np.uint8).reshape(k // 512, 16, n))


def unpack_weight(words, scales, fmt):
    g, _, n = scales.shape
    words = np.ascontiguousarray(words).reshape(g, 128, n, -1)
    if fmt == "e4m3":
        vals = words.view(ml_dtypes.float8_e4m3fn).astype(np.float64)
    else:
        nib = np.empty((g, 128, n, 4), np.uint8)
        nib[..., 0::2] = words & 0xF
        nib[..., 1::2] = words >> 4
        vals = E2M1[nib]
    vals = vals * np.repeat(np.exp2(scales.astype(np.float64) - 127.0), 8, axis=1)[..., None]
    return vals.transpose(0, 1, 3, 2).reshape(g * 512, n)


K, J, R, T, U, V, Z, M, O, C, N = 512, 256, 512, 1024, 1024, 1024, 512, 1024, 128, 512, 256


def setup_inputs():
    n = np.random.standard_normal
    idx = np.stack([np.random.permutation(T)[:J] for _ in range(8)])
    idx2 = np.stack([np.random.permutation(U)[:J] for _ in range(8)])
    idx3 = np.stack([np.random.permutation(V)[:J] for _ in range(8)])
    idx4 = np.random.permutation(M)[:J]
    idx5 = np.stack([np.random.permutation(C)[:J] for _ in range(8)])
    idx6 = np.stack([np.random.permutation(C)[:O] for _ in range(8)])
    idx7 = np.stack([np.random.permutation(J)[:O] for _ in range(8)])
    fk = mx_kscale(K)
    fr = mx_kscale(R)
    fz = mx_kscale(Z)
    wp = pack_weight(n((K, R)) * 1 / np.sqrt(K) / fk[:, None] * fr, "e2m1")
    xop = pack_weight(n((Z, M)) / fz[:, None], "e2m1")
    w2p = pack_weight(n((Z, R)) * 1 / np.sqrt(Z) * fz[:, None] * fr, "e4m3")
    wbp = pack_weight(n((R, N)) * 1 / np.sqrt(R) / fr[:, None], "e4m3")
    return {
        "ta": (np.random.randint(-7, 8, (K, T)).astype(np.float64)).astype(np.float32),
        "ga": ((np.random.randint(8, 19, (K, 1)) / 64.0) * fk[:, None]).astype(np.float32),
        "tb": (np.random.randint(-7, 8, (K, U)).astype(np.float64)).astype(np.float32),
        "gb": ((np.random.randint(4, 11, (K, 1)) / 64.0) * fk[:, None]).astype(np.float32),
        "td": (np.random.randint(-7, 8, (K, V)).astype(np.float64)).astype(np.float32),
        "gd": ((np.random.randint(2, 8, (K, 1)) / 64.0) * fk[:, None]).astype(np.float32),
        "w_words": wp[0],
        "w_scales": wp[1],
        "xo_words": xop[0],
        "xo_scales": xop[1],
        "w2_words": w2p[0],
        "w2_scales": w2p[1],
        "sa": (np.random.uniform(0.5, 1.6, (R, 1))).astype(np.float32),
        "sb": (np.random.uniform(0.5, 1.6, (R, 1))).astype(np.float32),
        "wb_words": wbp[0],
        "wb_scales": wbp[1],
        "offs": striped8(idx),
        "offs2": striped8(idx2),
        "offs3": striped8(idx3),
        "offs4": striped(idx4),
        "offs5": striped8(idx5),
        "offs6": striped8(idx6),
        "offs7": striped8(idx7),
    }


def reference(ta, ga, tb, gb, td, gd, w_words, w_scales, xo_words, xo_scales, w2_words, w2_scales, sa, sb, wb_words, wb_scales, offs, offs2, offs3, offs4, offs5, offs6, offs7):
    idx = unstriped8(offs)
    idx2 = unstriped8(offs2)
    idx3 = unstriped8(offs3)
    idx4 = unstriped(offs4)
    idx5 = unstriped8(offs5)
    idx6 = unstriped8(offs6)
    idx7 = unstriped8(offs7)
    wu = unpack_weight(w_words, w_scales, "e2m1")
    xou = unpack_weight(xo_words, xo_scales, "e2m1")
    w2u = unpack_weight(w2_words, w2_scales, "e4m3")
    wbu = unpack_weight(wb_words, wb_scales, "e4m3")
    xc = pick8(f64(ta), idx, 64) * f64(ga) + pick8(f64(tb), idx2, 64) * f64(gb) + pick8(f64(td), idx3, 64) * f64(gd)
    xcq = mxq(xc, 0, "e4m3")
    a = wu.T @ xcq
    xoidx4g = xou[:, idx4]
    b = w2u.T @ xoidx4g
    pw = np.zeros((R, C))
    pw[np.arange(R)[:, None], idx5[np.arange(R) % 512 // 64]] = a
    hid = np.abs(pick8(pw, idx6, 64) * f64(sa) - pick8(b, idx7, 64) * f64(sb))
    hidq = mxq(hid, 0, "e4m3")
    y = wbu.T @ hidq
    return y

@@ -1,0 +1,227 @@
+from contextlib import ExitStack
+
+import concourse.mybir as mybir
+
+K, J, R, T, Z, M, O, C, N = 512, 256, 512, 1024, 512, 1024, 128, 512, 256
+FLOPS = 2 * (K * R * J + Z * R * J + R * N * O)
+
+F32 = mybir.dt.float32
+BF16 = mybir.dt.bfloat16
+I32 = mybir.dt.int32
+U32 = mybir.dt.uint32
+U16 = mybir.dt.uint16
+U8 = mybir.dt.uint8
+FP8X4 = mybir.dt.float8_e4m3fn_x4
+FP4X4 = mybir.dt.float4_e2m1fn_x4
+ACT = mybir.ActivationFunctionType
+ALU = mybir.AluOpType
+
+P = 128
+PACK = 4
+HALF = J // 2
+O_VEC = 64
+
+
+def tile_picked_threebooks_plain_two_boardmeet_one_plain_kernel(
+    tc, ta, ga, tb, gb, td, gd, w_words, w_scales, xo_words, xo_scales, w2_words, w2_scales, sa, sb,
+    wb_words, wb_scales, offs, offs2, offs3, offs4, offs5, offs6, offs7, out,
+):
+    nc = tc.nc
+    with ExitStack() as ctx:
+        keep = ctx.enter_context(tc.tile_pool(name="keep", bufs=1))
+        psum = ctx.enter_context(tc.psum_pool(name="psum", bufs=1))
+
+        def tile(name, shape, dtype):
+            return keep.tile(shape, dtype, name=name, align_bytes=64)
+
+        def load_list(name, src):
+            lst = keep.tile(list(src.shape), U16, name=name)
+            nc.sync.dma_start(lst[:], src)
+            return lst
+
+        def load_column(name, src):
+            col = tile(name, [P, PACK], F32)
+            nc.gpsimd.dma_start(col[:], src.rearrange("(p t) o -> p (t o)", t=PACK))
+            return col
+
+        def load_table(name, src, t):
+            rows = tile(name + str(t), [P, T], F32)
+            nc.sync.dma_start(rows[:], src.rearrange("(p t) c -> p t c", t=PACK)[:, t, :])
+            return rows
+
+        def load_words(name, src, width, dtype):
+            words = tile(name, [P, width], dtype)
+            nc.sync.dma_start(words[:].bitcast(I32), src.bitcast(I32))
+            return words
+
+        def load_scales(name, src, width):
+            stage = tile(name + "_stage", [P, 2 * width], U8)
+            plane = tile(name + "_plane", [P, width], U8)
+            nc.vector.memset(plane[:].bitcast(I32), 0)
+            for h in range(2):
+                nc.sync.dma_start(
+                    stage[64 * h : 64 * h + 4, :].bitcast(I32).rearrange("r (q c) -> r q c", q=2),
+                    src[0, 8 * h : 8 * h + 8, :].bitcast(I32).rearrange("(q r) c -> r q c", q=2),
+                )
+            for q in range(4):
+                first = 64 * (q // 2)
+                nc.vector.tensor_copy(
+                    plane[32 * q : 32 * q + 4, :].bitcast(I32),
+                    stage[first : first + 4, (q % 2) * width : (q % 2 + 1) * width].bitcast(I32),
+                )
+            return plane
+
+        def deal(copy, name, src, dtype):
+            dealt = tile(name, [P, R], dtype)
+            copy(dealt[:].rearrange("p (t m) -> p t m", t=PACK), src[:].rearrange("p (m t) -> p t m", t=PACK))
+            return dealt
+
+        def fetch(dst, window, lst, scale):
+            nc.scalar.activation(dst, window[:].indirect(lst[:]), ACT.Copy, scale=scale)
+
+        board = [tile("board" + str(t), [P, C], F32) for t in range(PACK)]
+        for t in range(PACK):
+            nc.vector.memset(board[t][:], 0.0)
+
+        xc = tile("xc", [P, J, PACK], BF16)
+        xc_codes = tile("xc_codes", [P, J], U32)
+        xc_scales = tile("xc_scales", [P, J], U8)
+
+        def add_books(t, rows):
+            got = tile("got" + str(t), [P, 3, J], F32)
+            two = tile("two" + str(t), [P, J], F32)
+            for i in range(3):
+                fetch(got[:, i, :], rows[i], lists[i], steps[i][:, t : t + 1])
+            nc.vector.tensor_tensor(two[:], got[:, 0, :], got[:, 1, :], ALU.add)
+            cuts = [(0, J)] if t < PACK - 1 else [(0, HALF), (HALF, J)]
+            for lo, hi in cuts:
+                nc.vector.tensor_tensor(xc[:, lo:hi, t], two[:, lo:hi], got[:, 2, lo:hi], ALU.add)
+
+        steps = [load_column("ga_col", ga), load_column("gb_col", gb), load_column("gd_col", gd)]
+        sb_col = load_column("sb_col", sb)
+        sa_col = load_column("sa_col", sa)
+
+        xo_w = load_words("xo_w", xo_words[0], M, U16)
+        rows0 = [load_table("ta", ta, 0)]
+        note_list = load_list("note_list", offs4)
+        xo_s = load_scales("xo_s", xo_scales, M)
+        rows0.append(load_table("tb", tb, 0))
+        lists = [load_list("ta_list", offs)]
+        w2_w = load_words("w2_w", w2_words[0].rearrange("p c t -> p (c t)"), R, U32)
+        w2_s = load_scales("w2_s", w2_scales, R)
+        rows0.append(load_table("td", td, 0))
+        lists.append(load_list("tb_list", offs2))
+        lists.append(load_list("td_list", offs3))
+        rows1 = [load_table("ta", ta, 1)]
+        w_w = load_words("w_w", w_words[0], R, U16)
+        w_s = load_scales("w_s", w_scales, R)
+        rows1.append(load_table("tb", tb, 1))
+        slot_list = load_list("slot_list", offs7)
+        rows1.append(load_table("td", td, 1))
+        rows2 = [load_table("ta", ta, 2), load_table("tb", tb, 2), load_table("td", td, 2)]
+        rows3 = [load_table("ta", ta, 3), load_table("tb", tb, 3), load_table("td", td, 3)]
+        put_list = load_list("put_list", offs5)
+        place_list = load_list("place_list", offs6)
+        wb_w = load_words("wb_w", wb_words[0].rearrange("p c t -> p (c t)"), N, U32)
+        wb_s = load_scales("wb_s", wb_scales, N)
+
+        notes_w = tile("notes_w", [P, J], U16)
+        notes_s = tile("notes_s", [P, J], U8)
+        nc.vector.tensor_copy(notes_w[:], xo_w[:].indirect(note_list[:]))
+        nc.vector.tensor_copy(notes_s[:], xo_s[:].indirect(note_list[:]))
+        w2_wd = deal(nc.vector.tensor_copy, "w2_wd", w2_w, U32)
+        w2_sd = deal(nc.vector.tensor_copy, "w2_sd", w2_s, U8)
+        add_books(0, rows0)
+
+        second = tile("second", [P, PACK, O], F32)
+        for pair in range(2):
+            bank = psum.tile([P, 2, J], F32, name="b_bank" + str(pair))
+            for i in range(2):
+                cols = slice(P * (2 * pair + i), P * (2 * pair + i + 1))
+                nc.tensor.matmul_mx(
+                    out=bank[:, i, :], lhsT=w2_wd[:, cols].bitcast(FP8X4), lhsT_scale=w2_sd[:, cols],
+                    rhs=notes_w[:].bitcast(FP4X4), rhs_scale=notes_s[:], start=True, stop=True,
+                )
+            for i in range(2):
+                t = 2 * pair + i
+                b_rows = tile("b_rows" + str(t), [P, J], F32)
+                nc.scalar.copy(b_rows[:], bank[:, i, :])
+                fetch(second[:, t, :], b_rows, slot_list, sb_col[:, t : t + 1])
+
+        w_wd = deal(nc.scalar.copy, "w_wd", w_w, U16)
+        w_sd = deal(nc.vector.tensor_copy, "w_sd", w_s, U8)
+        add_books(1, rows1)
+        add_books(2, rows2)
+        add_books(3, rows3)
+
+        banks = [psum.tile([P, J], F32, name="a_bank" + str(i)) for i in range(5)]
+
+        def a_place(t, h):
+            if t >= 2:
+                return banks[t + 1][:, h * HALF : (h + 1) * HALF]
+            if h == 0:
+                return banks[t][:, 0:HALF]
+            return banks[2][:, t * HALF : (t + 1) * HALF]
+
+        for h in range(2):
+            slots = slice(h * HALF, (h + 1) * HALF)
+            nc.vector.quantize_mx(
+                out=xc_codes[:, slots].bitcast(FP8X4), scales=xc_scales[:, slots],
+                in_=xc[:, slots, :].rearrange("p j t -> p (j t)"),
+            )
+            for t in range(PACK):
+                cols = slice(P * t, P * (t + 1))
+                nc.tensor.matmul_mx(
+                    out=a_place(t, h), lhsT=w_wd[:, cols].bitcast(FP4X4), lhsT_scale=w_sd[:, cols],
+                    rhs=xc_codes[:, slots].bitcast(FP8X4), rhs_scale=xc_scales[:, slots], start=True, stop=True,
+                )
+
+        a_rows = tile("a_rows", [P, PACK, J], F32)
+        nc.scalar.copy(a_rows[:, 0, 0:HALF], banks[0][:, 0:HALF])
+        nc.scalar.copy(a_rows[:, 1, 0:HALF], banks[1][:, 0:HALF])
+        nc.scalar.copy(a_rows[:, 0:2, HALF:J], banks[2][:].rearrange("p (t j) -> p t j", t=2))
+        nc.scalar.copy(a_rows[:, 2, :], banks[3][:])
+        nc.scalar.copy(a_rows[:, 3, :], banks[4][:])
+
+        for h in range(2):
+            for t in range(2):
+                nc.vector.tensor_copy(
+                    board[t][:].indirect(put_list[:, h * HALF // 16 : (h + 1) * HALF // 16]),
+                    a_rows[:, t, h * HALF : (h + 1) * HALF],
+                )
+        for t in range(2, PACK):
+            nc.vector.tensor_copy(board[t][:].indirect(put_list[:]), a_rows[:, t, :])
+
+        first = tile("first", [P, PACK, O], F32)
+        for t in range(PACK):
+            fetch(first[:, t, :], board[t], place_list, sa_col[:, t : t + 1])
+        diff = tile("diff", [P, PACK, O], F32)
+        nc.vector.tensor_tensor(diff[:, 0:3, :], first[:, 0:3, :], second[:, 0:3, :], ALU.subtract)
+        nc.vector.tensor_tensor(diff[:, 3, :], first[:, 3, :], second[:, 3, :], ALU.subtract)
+
+        hid = tile("hid", [P, O, PACK], BF16)
+        by_place = diff[:].rearrange("p t o -> p o t")
+        nc.vector.scalar_tensor_tensor(
+            hid[:, 0:O_VEC, :], by_place[:, 0:O_VEC, :], -1.0, by_place[:, 0:O_VEC, :], ALU.mult, ALU.max
+        )
+        nc.scalar.activation(hid[:, O_VEC:O, :], by_place[:, O_VEC:O, :], ACT.Abs)
+        hid_codes = tile("hid_codes", [P, O], U32)
+        hid_scales = tile("hid_scales", [P, O], U8)
+        nc.vector.quantize_mx(
+            out=hid_codes[:].bitcast(FP8X4), scales=hid_scales[:], in_=hid[:].rearrange("p o t -> p (o t)")
+        )
+
+        for i in range(2):
+            cols = slice(P * i, P * (i + 1))
+            bank = psum.tile([P, 2, J], F32, name="b_bank" + str(i))
+            nc.tensor.matmul_mx(
+                out=bank[:, 0, 0:O], lhsT=wb_w[:, cols].bitcast(FP8X4), lhsT_scale=wb_s[:, cols],
+                rhs=hid_codes[:].bitcast(FP8X4), rhs_scale=hid_scales[:], start=True, stop=True,
+            )
+            result = tile("result" + str(i), [P, O], F32)
+            if i == 0:
+                nc.vector.tensor_copy(result[:], bank[:, 0, 0:O])
+                nc.sync.dma_start(out[cols, :], result[:])
+            else:
+                nc.scalar.copy(result[:], bank[:, 0, 0:O])
+                nc.scalar.dma_start(out[cols, :], result[:])

@@ -19,7 +19,7 @@ ALU = mybir.AluOpType
 P = 128
 PACK = 4
 HALF = J // 2
-O_VEC = 64
+O_VEC = 48
 
 
 def tile_picked_threebooks_plain_two_boardmeet_one_plain_kernel(
@@ -41,7 +41,7 @@ def tile_picked_threebooks_plain_two_boardmeet_one_plain_kernel(
 
         def load_column(name, src):
             col = tile(name, [P, PACK], F32)
-            nc.gpsimd.dma_start(col[:], src.rearrange("(p t) o -> p (t o)", t=PACK))
+            nc.sync.dma_start(col[:], src.rearrange("(p t) o -> p (t o)", t=PACK))
             return col
 
         def load_table(name, src, t):
@@ -54,22 +54,24 @@ def tile_picked_threebooks_plain_two_boardmeet_one_plain_kernel(
             nc.sync.dma_start(words[:].bitcast(I32), src.bitcast(I32))
             return words
 
-        def load_scales(name, src, width):
+        def scale_plane(name, width):
             stage = tile(name + "_stage", [P, 2 * width], U8)
             plane = tile(name + "_plane", [P, width], U8)
             nc.vector.memset(plane[:].bitcast(I32), 0)
-            for h in range(2):
-                nc.sync.dma_start(
-                    stage[64 * h : 64 * h + 4, :].bitcast(I32).rearrange("r (q c) -> r q c", q=2),
-                    src[0, 8 * h : 8 * h + 8, :].bitcast(I32).rearrange("(q r) c -> r q c", q=2),
-                )
-            for q in range(4):
-                first = 64 * (q // 2)
+            return stage, plane, width
+
+        def load_scales(tiles, src, h):
+            stage, plane, width = tiles
+            nc.sync.dma_start(
+                stage[64 * h : 64 * h + 4, :].bitcast(I32).rearrange("r (q c) -> r q c", q=2),
+                src[0, 8 * h : 8 * h + 8, :].bitcast(I32).rearrange("(q r) c -> r q c", q=2),
+            )
+            for q in range(2):
+                first = 64 * h + 32 * q
                 nc.vector.tensor_copy(
-                    plane[32 * q : 32 * q + 4, :].bitcast(I32),
-                    stage[first : first + 4, (q % 2) * width : (q % 2 + 1) * width].bitcast(I32),
+                    plane[first : first + 4, :].bitcast(I32),
+                    stage[64 * h : 64 * h + 4, q * width : (q + 1) * width].bitcast(I32),
                 )
-            return plane
 
         def deal(copy, name, src, dtype):
             dealt = tile(name, [P, R], dtype)
@@ -93,68 +95,63 @@ def tile_picked_threebooks_plain_two_boardmeet_one_plain_kernel(
             for i in range(3):
                 fetch(got[:, i, :], rows[i], lists[i], steps[i][:, t : t + 1])
             nc.vector.tensor_tensor(two[:], got[:, 0, :], got[:, 1, :], ALU.add)
-            cuts = [(0, J)] if t < PACK - 1 else [(0, HALF), (HALF, J)]
-            for lo, hi in cuts:
-                nc.vector.tensor_tensor(xc[:, lo:hi, t], two[:, lo:hi], got[:, 2, lo:hi], ALU.add)
+            if t < PACK - 1:
+                nc.vector.tensor_tensor(xc[:, :, t], two[:], got[:, 2, :], ALU.add)
+            return two, got
 
-        steps = [load_column("ga_col", ga), load_column("gb_col", gb), load_column("gd_col", gd)]
-        sb_col = load_column("sb_col", sb)
-        sa_col = load_column("sa_col", sa)
-
-        xo_w = load_words("xo_w", xo_words[0], M, U16)
         rows0 = [load_table("ta", ta, 0)]
-        note_list = load_list("note_list", offs4)
-        xo_s = load_scales("xo_s", xo_scales, M)
-        rows0.append(load_table("tb", tb, 0))
         lists = [load_list("ta_list", offs)]
-        w2_w = load_words("w2_w", w2_words[0].rearrange("p c t -> p (c t)"), R, U32)
-        w2_s = load_scales("w2_s", w2_scales, R)
-        rows0.append(load_table("td", td, 0))
+        steps = [load_column("ga_col", ga)]
+        xo_w = load_words("xo_w", xo_words[0], M, U16)
+        xo_s = scale_plane("xo_s", M)
+        load_scales(xo_s, xo_scales, 0)
+        load_scales(xo_s, xo_scales, 1)
+        rows0.append(load_table("tb", tb, 0))
         lists.append(load_list("tb_list", offs2))
+        steps.append(load_column("gb_col", gb))
+        note_list = load_list("note_list", offs4)
+        rows0.append(load_table("td", td, 0))
         lists.append(load_list("td_list", offs3))
+        steps.append(load_column("gd_col", gd))
+        w2_s = scale_plane("w2_s", R)
+        load_scales(w2_s, w2_scales, 0)
         rows1 = [load_table("ta", ta, 1)]
-        w_w = load_words("w_w", w_words[0], R, U16)
-        w_s = load_scales("w_s", w_scales, R)
+        load_scales(w2_s, w2_scales, 1)
+        w_s = scale_plane("w_s", R)
+        load_scales(w_s, w_scales, 0)
         rows1.append(load_table("tb", tb, 1))
-        slot_list = load_list("slot_list", offs7)
+        load_scales(w_s, w_scales, 1)
         rows1.append(load_table("td", td, 1))
-        rows2 = [load_table("ta", ta, 2), load_table("tb", tb, 2), load_table("td", td, 2)]
-        rows3 = [load_table("ta", ta, 3), load_table("tb", tb, 3), load_table("td", td, 3)]
+        wb_s = scale_plane("wb_s", N)
+        load_scales(wb_s, wb_scales, 0)
+        load_scales(wb_s, wb_scales, 1)
+        rows2 = [load_table("ta", ta, 2)]
         put_list = load_list("put_list", offs5)
+        rows2.extend([load_table("tb", tb, 2), load_table("td", td, 2)])
+        rows3 = [load_table("ta", ta, 3), load_table("tb", tb, 3), load_table("td", td, 3)]
+        w_w = load_words("w_w", w_words[0], R, U16)
+        w2_w = load_words("w2_w", w2_words[0].rearrange("p c t -> p (c t)"), R, U32)
+        slot_list = load_list("slot_list", offs7)
+        sb_col = load_column("sb_col", sb)
         place_list = load_list("place_list", offs6)
+        sa_col = load_column("sa_col", sa)
         wb_w = load_words("wb_w", wb_words[0].rearrange("p c t -> p (c t)"), N, U32)
-        wb_s = load_scales("wb_s", wb_scales, N)
 
         notes_w = tile("notes_w", [P, J], U16)
         notes_s = tile("notes_s", [P, J], U8)
         nc.vector.tensor_copy(notes_w[:], xo_w[:].indirect(note_list[:]))
-        nc.vector.tensor_copy(notes_s[:], xo_s[:].indirect(note_list[:]))
-        w2_wd = deal(nc.vector.tensor_copy, "w2_wd", w2_w, U32)
-        w2_sd = deal(nc.vector.tensor_copy, "w2_sd", w2_s, U8)
+        nc.vector.tensor_copy(notes_s[:], xo_s[1][:].indirect(note_list[:]))
         add_books(0, rows0)
-
-        second = tile("second", [P, PACK, O], F32)
-        for pair in range(2):
-            bank = psum.tile([P, 2, J], F32, name="b_bank" + str(pair))
-            for i in range(2):
-                cols = slice(P * (2 * pair + i), P * (2 * pair + i + 1))
-                nc.tensor.matmul_mx(
-                    out=bank[:, i, :], lhsT=w2_wd[:, cols].bitcast(FP8X4), lhsT_scale=w2_sd[:, cols],
-                    rhs=notes_w[:].bitcast(FP4X4), rhs_scale=notes_s[:], start=True, stop=True,
-                )
-            for i in range(2):
-                t = 2 * pair + i
-                b_rows = tile("b_rows" + str(t), [P, J], F32)
-                nc.scalar.copy(b_rows[:], bank[:, i, :])
-                fetch(second[:, t, :], b_rows, slot_list, sb_col[:, t : t + 1])
-
-        w_wd = deal(nc.scalar.copy, "w_wd", w_w, U16)
-        w_sd = deal(nc.vector.tensor_copy, "w_sd", w_s, U8)
+        w2_sd = deal(nc.vector.tensor_copy, "w2_sd", w2_s[1], U8)
+        w_sd = deal(nc.vector.tensor_copy, "w_sd", w_s[1], U8)
         add_books(1, rows1)
         add_books(2, rows2)
-        add_books(3, rows3)
+        two, last = add_books(3, rows3)
+        w_wd = deal(nc.scalar.copy, "w_wd", w_w, U16)
+        w2_wd = tile("w2_wd", [P, R], U32)
+        nc.scalar.copy(w2_wd[:].rearrange("p (t m) -> p m t", t=PACK), w2_w[:].rearrange("p (m t) -> p m t", t=PACK))
 
-        banks = [psum.tile([P, J], F32, name="a_bank" + str(i)) for i in range(5)]
+        banks = [psum.tile([P, J], F32, name="bank" + str(i)) for i in range(5)]
 
         def a_place(t, h):
             if t >= 2:
@@ -165,6 +162,7 @@ def tile_picked_threebooks_plain_two_boardmeet_one_plain_kernel(
 
         for h in range(2):
             slots = slice(h * HALF, (h + 1) * HALF)
+            nc.vector.tensor_tensor(xc[:, slots, PACK - 1], two[:, slots], last[:, 2, slots], ALU.add)
             nc.vector.quantize_mx(
                 out=xc_codes[:, slots].bitcast(FP8X4), scales=xc_scales[:, slots],
                 in_=xc[:, slots, :].rearrange("p j t -> p (j t)"),
@@ -182,6 +180,21 @@ def tile_picked_threebooks_plain_two_boardmeet_one_plain_kernel(
         nc.scalar.copy(a_rows[:, 0:2, HALF:J], banks[2][:].rearrange("p (t j) -> p t j", t=2))
         nc.scalar.copy(a_rows[:, 2, :], banks[3][:])
         nc.scalar.copy(a_rows[:, 3, :], banks[4][:])
+
+        second = tile("second", [P, PACK, O], F32)
+        for pair in range(2):
+            bank = psum.tile([P, 2, J], F32, name="bank" + str(pair))
+            for i in range(2):
+                cols = slice(P * (2 * pair + i), P * (2 * pair + i + 1))
+                nc.tensor.matmul_mx(
+                    out=bank[:, i, :], lhsT=w2_wd[:, cols].bitcast(FP8X4), lhsT_scale=w2_sd[:, cols],
+                    rhs=notes_w[:].bitcast(FP4X4), rhs_scale=notes_s[:], start=True, stop=True,
+                )
+            for i in range(2):
+                t = 2 * pair + i
+                b_rows = tile("b_rows" + str(t), [P, J], F32)
+                nc.scalar.copy(b_rows[:], bank[:, i, :])
+                fetch(second[:, t, :], b_rows, slot_list, sb_col[:, t : t + 1])
 
         for h in range(2):
             for t in range(2):
@@ -204,7 +217,11 @@ def tile_picked_threebooks_plain_two_boardmeet_one_plain_kernel(
         nc.vector.scalar_tensor_tensor(
             hid[:, 0:O_VEC, :], by_place[:, 0:O_VEC, :], -1.0, by_place[:, 0:O_VEC, :], ALU.mult, ALU.max
         )
-        nc.scalar.activation(hid[:, O_VEC:O, :], by_place[:, O_VEC:O, :], ACT.Abs)
+        nc.scalar.activation(
+            hid[:, O_VEC:O, :].rearrange("p (c i) t -> p c t i", i=4),
+            diff[:, :, O_VEC:O].rearrange("p t (c i) -> p c t i", i=4),
+            ACT.Abs,
+        )
         hid_codes = tile("hid_codes", [P, O], U32)
         hid_scales = tile("hid_scales", [P, O], U8)
         nc.vector.quantize_mx(
@@ -213,15 +230,15 @@ def tile_picked_threebooks_plain_two_boardmeet_one_plain_kernel(
 
         for i in range(2):
             cols = slice(P * i, P * (i + 1))
-            bank = psum.tile([P, 2, J], F32, name="b_bank" + str(i))
+            bank = psum.tile([P, O], F32, name="out_bank" + str(i))
             nc.tensor.matmul_mx(
-                out=bank[:, 0, 0:O], lhsT=wb_w[:, cols].bitcast(FP8X4), lhsT_scale=wb_s[:, cols],
+                out=bank[:], lhsT=wb_w[:, cols].bitcast(FP8X4), lhsT_scale=wb_s[1][:, cols],
                 rhs=hid_codes[:].bitcast(FP8X4), rhs_scale=hid_scales[:], start=True, stop=True,
             )
             result = tile("result" + str(i), [P, O], F32)
             if i == 0:
-                nc.vector.tensor_copy(result[:], bank[:, 0, 0:O])
+                nc.vector.tensor_copy(result[:], bank[:])
                 nc.sync.dma_start(out[cols, :], result[:])
             else:
-                nc.scalar.copy(result[:], bank[:, 0, 0:O])
+                nc.scalar.copy(result[:], bank[:])
                 nc.scalar.dma_start(out[cols, :], result[:])

@@ -60,9 +60,9 @@ def tile_picked_threebooks_plain_two_boardmeet_one_plain_kernel(
             nc.vector.memset(plane[:].bitcast(I32), 0)
             return stage, plane, width
 
-        def load_scales(tiles, src, h):
+        def load_scales(queue, tiles, src, h):
             stage, plane, width = tiles
-            nc.sync.dma_start(
+            queue.dma_start(
                 stage[64 * h : 64 * h + 4, :].bitcast(I32).rearrange("r (q c) -> r q c", q=2),
                 src[0, 8 * h : 8 * h + 8, :].bitcast(I32).rearrange("(q r) c -> r q c", q=2),
             )
@@ -89,64 +89,65 @@ def tile_picked_threebooks_plain_two_boardmeet_one_plain_kernel(
         xc_codes = tile("xc_codes", [P, J], U32)
         xc_scales = tile("xc_scales", [P, J], U8)
 
-        def add_books(t, rows):
-            got = tile("got" + str(t), [P, 3, J], F32)
-            two = tile("two" + str(t), [P, J], F32)
-            for i in range(3):
-                fetch(got[:, i, :], rows[i], lists[i], steps[i][:, t : t + 1])
-            nc.vector.tensor_tensor(two[:], got[:, 0, :], got[:, 1, :], ALU.add)
-            if t < PACK - 1:
-                nc.vector.tensor_tensor(xc[:, :, t], two[:], got[:, 2, :], ALU.add)
-            return two, got
+        got = [tile("got" + str(t), [P, 3, J], F32) for t in range(PACK)]
+        two = [tile("two" + str(t), [P, J], F32) for t in range(PACK)]
 
-        rows0 = [load_table("ta", ta, 0)]
-        lists = [load_list("ta_list", offs)]
-        steps = [load_column("ga_col", ga)]
-        xo_w = load_words("xo_w", xo_words[0], M, U16)
+        def fetch_book(i, t, rows):
+            fetch(got[t][:, i, :], rows[i], lists[i], steps[i][:, t : t + 1])
+            if i == 1:
+                nc.vector.tensor_tensor(two[t][:], got[t][:, 0, :], got[t][:, 1, :], ALU.add)
+
+        def add_third(t, slots):
+            nc.vector.tensor_tensor(xc[:, slots, t], two[t][:, slots], got[t][:, 2, slots], ALU.add)
+
         xo_s = scale_plane("xo_s", M)
-        load_scales(xo_s, xo_scales, 0)
-        load_scales(xo_s, xo_scales, 1)
-        rows0.append(load_table("tb", tb, 0))
-        lists.append(load_list("tb_list", offs2))
-        steps.append(load_column("gb_col", gb))
-        note_list = load_list("note_list", offs4)
-        rows0.append(load_table("td", td, 0))
-        lists.append(load_list("td_list", offs3))
-        steps.append(load_column("gd_col", gd))
         w2_s = scale_plane("w2_s", R)
-        load_scales(w2_s, w2_scales, 0)
-        rows1 = [load_table("ta", ta, 1)]
-        load_scales(w2_s, w2_scales, 1)
         w_s = scale_plane("w_s", R)
-        load_scales(w_s, w_scales, 0)
-        rows1.append(load_table("tb", tb, 1))
-        load_scales(w_s, w_scales, 1)
-        rows1.append(load_table("td", td, 1))
-        wb_s = scale_plane("wb_s", N)
-        load_scales(wb_s, wb_scales, 0)
-        load_scales(wb_s, wb_scales, 1)
+        for tiles, src in ((w_s, w_scales), (xo_s, xo_scales)):
+            for h in range(2):
+                load_scales(nc.gpsimd, tiles, src, h)
+        rows0, rows1, lists, steps = [], [], [], []
+        for name, table, lst, step in (("ta", ta, offs, ga), ("tb", tb, offs2, gb), ("td", td, offs3, gd)):
+            rows0.append(load_table(name, table, 0))
+            lists.append(load_list(name + "_list", lst))
+            rows1.append(load_table(name, table, 1))
+            steps.append(load_column(name + "_step", step))
+        for h in range(2):
+            load_scales(nc.sync, w2_s, w2_scales, h)
         rows2 = [load_table("ta", ta, 2)]
-        put_list = load_list("put_list", offs5)
+        note_list = load_list("note_list", offs4)
+        xo_w = load_words("xo_w", xo_words[0], M, U16)
         rows2.extend([load_table("tb", tb, 2), load_table("td", td, 2)])
         rows3 = [load_table("ta", ta, 3), load_table("tb", tb, 3), load_table("td", td, 3)]
         w_w = load_words("w_w", w_words[0], R, U16)
+        put_list = load_list("put_list", offs5)
         w2_w = load_words("w2_w", w2_words[0].rearrange("p c t -> p (c t)"), R, U32)
         slot_list = load_list("slot_list", offs7)
         sb_col = load_column("sb_col", sb)
         place_list = load_list("place_list", offs6)
         sa_col = load_column("sa_col", sa)
         wb_w = load_words("wb_w", wb_words[0].rearrange("p c t -> p (c t)"), N, U32)
+        wb_s = tile("wb_s", [P, N], U8)
+        nc.vector.memset(wb_s[:].bitcast(I32), 0)
+        for q in range(4):
+            nc.sync.dma_start(wb_s[32 * q : 32 * q + 4, :].bitcast(I32), wb_scales[0, 4 * q : 4 * q + 4, :].bitcast(I32))
 
+        w_sd = deal(nc.vector.tensor_copy, "w_sd", w_s[1], U8)
+        for i in range(3):
+            fetch_book(i, 0, rows0)
+            fetch_book(i, 1, rows1)
+        add_third(0, slice(0, J))
+        add_third(1, slice(0, J))
+        w2_sd = deal(nc.vector.tensor_copy, "w2_sd", w2_s[1], U8)
         notes_w = tile("notes_w", [P, J], U16)
         notes_s = tile("notes_s", [P, J], U8)
         nc.vector.tensor_copy(notes_w[:], xo_w[:].indirect(note_list[:]))
         nc.vector.tensor_copy(notes_s[:], xo_s[1][:].indirect(note_list[:]))
-        add_books(0, rows0)
-        w2_sd = deal(nc.vector.tensor_copy, "w2_sd", w2_s[1], U8)
-        w_sd = deal(nc.vector.tensor_copy, "w_sd", w_s[1], U8)
-        add_books(1, rows1)
-        add_books(2, rows2)
-        two, last = add_books(3, rows3)
+        for i in range(3):
+            fetch_book(i, 2, rows2)
+        add_third(2, slice(0, J))
+        for i in range(3):
+            fetch_book(i, 3, rows3)
         w_wd = deal(nc.scalar.copy, "w_wd", w_w, U16)
         w2_wd = tile("w2_wd", [P, R], U32)
         nc.scalar.copy(w2_wd[:].rearrange("p (t m) -> p m t", t=PACK), w2_w[:].rearrange("p (m t) -> p m t", t=PACK))
@@ -162,7 +163,7 @@ def tile_picked_threebooks_plain_two_boardmeet_one_plain_kernel(
 
         for h in range(2):
             slots = slice(h * HALF, (h + 1) * HALF)
-            nc.vector.tensor_tensor(xc[:, slots, PACK - 1], two[:, slots], last[:, 2, slots], ALU.add)
+            add_third(PACK - 1, slots)
             nc.vector.quantize_mx(
                 out=xc_codes[:, slots].bitcast(FP8X4), scales=xc_scales[:, slots],
                 in_=xc[:, slots, :].rearrange("p j t -> p (j t)"),
@@ -232,7 +233,7 @@ def tile_picked_threebooks_plain_two_boardmeet_one_plain_kernel(
             cols = slice(P * i, P * (i + 1))
             bank = psum.tile([P, O], F32, name="out_bank" + str(i))
             nc.tensor.matmul_mx(
-                out=bank[:], lhsT=wb_w[:, cols].bitcast(FP8X4), lhsT_scale=wb_s[1][:, cols],
+                out=bank[:], lhsT=wb_w[:, cols].bitcast(FP8X4), lhsT_scale=wb_s[:, cols],
                 rhs=hid_codes[:].bitcast(FP8X4), rhs_scale=hid_scales[:], start=True, stop=True,
             )
             result = tile("result" + str(i), [P, O], F32)

@@ -54,33 +54,36 @@ def tile_picked_threebooks_plain_two_boardmeet_one_plain_kernel(
             nc.sync.dma_start(words[:].bitcast(I32), src.bitcast(I32))
             return words
 
-        def scale_plane(name, width):
-            stage = tile(name + "_stage", [P, 2 * width], U8)
-            plane = tile(name + "_plane", [P, width], U8)
-            nc.vector.memset(plane[:].bitcast(I32), 0)
-            return stage, plane, width
+        def zeroed(name, width, spare=0):
+            plane = tile(name, [P, width + spare], U8)
+            nc.vector.memset(plane[:, 0:width].bitcast(I32), 0)
+            return plane
 
-        def load_scales(queue, tiles, src, h):
-            stage, plane, width = tiles
-            queue.dma_start(
-                stage[64 * h : 64 * h + 4, :].bitcast(I32).rearrange("r (q c) -> r q c", q=2),
-                src[0, 8 * h : 8 * h + 8, :].bitcast(I32).rearrange("(q r) c -> r q c", q=2),
-            )
-            for q in range(2):
-                first = 64 * h + 32 * q
+        def load_scale_rows(plane, src, q):
+            nc.sync.dma_start(plane[32 * q : 32 * q + 4, :].bitcast(I32), src[0, 4 * q : 4 * q + 4, :].bitcast(I32))
+
+        def load_scale_halves(plane, src):
+            for h in range(2):
+                nc.gpsimd.dma_start(
+                    plane[64 * h : 64 * h + 4, :].bitcast(I32).rearrange("r (q c) -> r q c", q=2),
+                    src[0, 8 * h : 8 * h + 8, :].bitcast(I32).rearrange("(q r) c -> r q c", q=2),
+                )
                 nc.vector.tensor_copy(
-                    plane[first : first + 4, :].bitcast(I32),
-                    stage[64 * h : 64 * h + 4, q * width : (q + 1) * width].bitcast(I32),
+                    plane[64 * h + 32 : 64 * h + 36, 0:R].bitcast(I32), plane[64 * h : 64 * h + 4, R : 2 * R].bitcast(I32)
                 )
 
         def deal(copy, name, src, dtype):
             dealt = tile(name, [P, R], dtype)
-            copy(dealt[:].rearrange("p (t m) -> p t m", t=PACK), src[:].rearrange("p (m t) -> p t m", t=PACK))
+            copy(dealt[:].rearrange("p (t m) -> p t m", t=PACK), src[:, 0:R].rearrange("p (m t) -> p t m", t=PACK))
             return dealt
 
         def fetch(dst, window, lst, scale):
             nc.scalar.activation(dst, window[:].indirect(lst[:]), ACT.Copy, scale=scale)
 
+        xo_s = zeroed("xo_s", M)
+        w_s = zeroed("w_s", R, spare=R)
+        w2_s = zeroed("w2_s", R, spare=R)
+        wb_s = zeroed("wb_s", N)
         board = [tile("board" + str(t), [P, C], F32) for t in range(PACK)]
         for t in range(PACK):
             nc.vector.memset(board[t][:], 0.0)
@@ -88,37 +91,45 @@ def tile_picked_threebooks_plain_two_boardmeet_one_plain_kernel(
         xc = tile("xc", [P, J, PACK], BF16)
         xc_codes = tile("xc_codes", [P, J], U32)
         xc_scales = tile("xc_scales", [P, J], U8)
+        got = [[tile("got" + str(pair) + str(i), [P, 2, J], F32) for i in range(3)] for pair in range(2)]
+        two = [tile("two" + str(pair), [P, 2, J], F32) for pair in range(2)]
 
-        got = [tile("got" + str(t), [P, 3, J], F32) for t in range(PACK)]
-        two = [tile("two" + str(t), [P, J], F32) for t in range(PACK)]
+        def fetch_pair(pair):
+            for i in range(3):
+                for u in range(2):
+                    t = 2 * pair + u
+                    fetch(got[pair][i][:, u, :], rows[i][t], lists[i], steps[i][:, t : t + 1])
+                if i == 1:
+                    nc.vector.tensor_tensor(two[pair][:], got[pair][0][:], got[pair][1][:], ALU.add)
 
-        def fetch_book(i, t, rows):
-            fetch(got[t][:, i, :], rows[i], lists[i], steps[i][:, t : t + 1])
-            if i == 1:
-                nc.vector.tensor_tensor(two[t][:], got[t][:, 0, :], got[t][:, 1, :], ALU.add)
+        def add_third(pair, slots):
+            nc.vector.tensor_tensor(
+                xc[:, slots, 2 * pair : 2 * pair + 2].rearrange("p (c i) u -> p c u i", i=4),
+                two[pair][:, :, slots].rearrange("p u (c i) -> p c u i", i=4),
+                got[pair][2][:, :, slots].rearrange("p u (c i) -> p c u i", i=4),
+                ALU.add,
+            )
 
-        def add_third(t, slots):
-            nc.vector.tensor_tensor(xc[:, slots, t], two[t][:, slots], got[t][:, 2, slots], ALU.add)
-
-        xo_s = scale_plane("xo_s", M)
-        w2_s = scale_plane("w2_s", R)
-        w_s = scale_plane("w_s", R)
-        for tiles, src in ((w_s, w_scales), (xo_s, xo_scales)):
-            for h in range(2):
-                load_scales(nc.gpsimd, tiles, src, h)
-        rows0, rows1, lists, steps = [], [], [], []
-        for name, table, lst, step in (("ta", ta, offs, ga), ("tb", tb, offs2, gb), ("td", td, offs3, gd)):
-            rows0.append(load_table(name, table, 0))
+        load_scale_halves(w_s, w_scales)
+        load_scale_halves(w2_s, w2_scales)
+        books = (("ta", ta, offs, ga), ("tb", tb, offs2, gb), ("td", td, offs3, gd))
+        rows, lists, steps = [], [], []
+        for name, table, lst, step in books:
+            rows.append([load_table(name, table, 0)])
             lists.append(load_list(name + "_list", lst))
-            rows1.append(load_table(name, table, 1))
             steps.append(load_column(name + "_step", step))
-        for h in range(2):
-            load_scales(nc.sync, w2_s, w2_scales, h)
-        rows2 = [load_table("ta", ta, 2)]
+            rows[-1].append(load_table(name, table, 1))
+        load_scale_rows(xo_s, xo_scales, 0)
+        load_scale_rows(xo_s, xo_scales, 2)
+        rows[0].append(load_table("ta", ta, 2))
+        load_scale_rows(xo_s, xo_scales, 1)
+        load_scale_rows(xo_s, xo_scales, 3)
+        rows[0].append(load_table("ta", ta, 3))
         note_list = load_list("note_list", offs4)
         xo_w = load_words("xo_w", xo_words[0], M, U16)
-        rows2.extend([load_table("tb", tb, 2), load_table("td", td, 2)])
-        rows3 = [load_table("ta", ta, 3), load_table("tb", tb, 3), load_table("td", td, 3)]
+        for i in (1, 2):
+            for t in (2, 3):
+                rows[i].append(load_table(books[i][0], books[i][1], t))
         w_w = load_words("w_w", w_words[0], R, U16)
         put_list = load_list("put_list", offs5)
         w2_w = load_words("w2_w", w2_words[0].rearrange("p c t -> p (c t)"), R, U32)
@@ -127,27 +138,18 @@ def tile_picked_threebooks_plain_two_boardmeet_one_plain_kernel(
         place_list = load_list("place_list", offs6)
         sa_col = load_column("sa_col", sa)
         wb_w = load_words("wb_w", wb_words[0].rearrange("p c t -> p (c t)"), N, U32)
-        wb_s = tile("wb_s", [P, N], U8)
-        nc.vector.memset(wb_s[:].bitcast(I32), 0)
         for q in range(4):
-            nc.sync.dma_start(wb_s[32 * q : 32 * q + 4, :].bitcast(I32), wb_scales[0, 4 * q : 4 * q + 4, :].bitcast(I32))
+            load_scale_rows(wb_s, wb_scales, q)
 
-        w_sd = deal(nc.vector.tensor_copy, "w_sd", w_s[1], U8)
-        for i in range(3):
-            fetch_book(i, 0, rows0)
-            fetch_book(i, 1, rows1)
+        w_sd = deal(nc.vector.tensor_copy, "w_sd", w_s, U8)
+        w2_sd = deal(nc.vector.tensor_copy, "w2_sd", w2_s, U8)
+        fetch_pair(0)
         add_third(0, slice(0, J))
-        add_third(1, slice(0, J))
-        w2_sd = deal(nc.vector.tensor_copy, "w2_sd", w2_s[1], U8)
         notes_w = tile("notes_w", [P, J], U16)
         notes_s = tile("notes_s", [P, J], U8)
+        nc.vector.tensor_copy(notes_s[:], xo_s[:].indirect(note_list[:]))
         nc.vector.tensor_copy(notes_w[:], xo_w[:].indirect(note_list[:]))
-        nc.vector.tensor_copy(notes_s[:], xo_s[1][:].indirect(note_list[:]))
-        for i in range(3):
-            fetch_book(i, 2, rows2)
-        add_third(2, slice(0, J))
-        for i in range(3):
-            fetch_book(i, 3, rows3)
+        fetch_pair(1)
         w_wd = deal(nc.scalar.copy, "w_wd", w_w, U16)
         w2_wd = tile("w2_wd", [P, R], U32)
         nc.scalar.copy(w2_wd[:].rearrange("p (t m) -> p m t", t=PACK), w2_w[:].rearrange("p (m t) -> p m t", t=PACK))
@@ -163,7 +165,7 @@ def tile_picked_threebooks_plain_two_boardmeet_one_plain_kernel(
 
         for h in range(2):
             slots = slice(h * HALF, (h + 1) * HALF)
-            add_third(PACK - 1, slots)
+            add_third(1, slots)
             nc.vector.quantize_mx(
                 out=xc_codes[:, slots].bitcast(FP8X4), scales=xc_scales[:, slots],
                 in_=xc[:, slots, :].rearrange("p j t -> p (j t)"),

@@ -18,8 +18,11 @@ ALU = mybir.AluOpType
 
 P = 128
 PACK = 4
+QUADRANT = 32
+LIST_ROWS = 16
+LINE = 4
 HALF = J // 2
-O_VEC = 48
+PLACES_ON_VECTOR = 48
 
 
 def tile_picked_threebooks_plain_two_boardmeet_one_plain_kernel(
@@ -45,32 +48,46 @@ def tile_picked_threebooks_plain_two_boardmeet_one_plain_kernel(
             return col
 
         def load_table(name, src, t):
-            rows = tile(name + str(t), [P, T], F32)
-            nc.sync.dma_start(rows[:], src.rearrange("(p t) c -> p t c", t=PACK)[:, t, :])
-            return rows
+            window = tile(name + str(t), [P, T], F32)
+            nc.sync.dma_start(window[:], src.rearrange("(p t) c -> p t c", t=PACK)[:, t, :])
+            return window
 
         def load_words(name, src, width, dtype):
             words = tile(name, [P, width], dtype)
             nc.sync.dma_start(words[:].bitcast(I32), src.bitcast(I32))
             return words
 
-        def zeroed(name, width, spare=0):
-            plane = tile(name, [P, width + spare], U8)
-            nc.vector.memset(plane[:, 0:width].bitcast(I32), 0)
-            return plane
+        def scale_tile(name, width, spare=0):
+            scales = tile(name, [P, width + spare], U8)
+            nc.vector.memset(scales[:, 0:width].bitcast(I32), 0)
+            return scales
 
-        def load_scale_rows(plane, src, q):
-            nc.sync.dma_start(plane[32 * q : 32 * q + 4, :].bitcast(I32), src[0, 4 * q : 4 * q + 4, :].bitcast(I32))
+        def load_scale_pair(dst, src, h):
+            first = 2 * h * QUADRANT
+            nc.sync.dma_start(
+                dst[first : first + 4, :].bitcast(I32).rearrange("r (q c) -> r q c", q=2),
+                src[0, 8 * h : 8 * h + 8, :].bitcast(I32).rearrange("(q r) c -> r q c", q=2),
+            )
 
-        def load_scale_halves(plane, src):
+        def load_weight_scales(scales, src):
             for h in range(2):
-                nc.gpsimd.dma_start(
-                    plane[64 * h : 64 * h + 4, :].bitcast(I32).rearrange("r (q c) -> r q c", q=2),
-                    src[0, 8 * h : 8 * h + 8, :].bitcast(I32).rearrange("(q r) c -> r q c", q=2),
-                )
+                load_scale_pair(scales, src, h)
+                even, odd = 2 * h * QUADRANT, (2 * h + 1) * QUADRANT
                 nc.vector.tensor_copy(
-                    plane[64 * h + 32 : 64 * h + 36, 0:R].bitcast(I32), plane[64 * h : 64 * h + 4, R : 2 * R].bitcast(I32)
+                    scales[odd : odd + 4, 0:R].bitcast(I32), scales[even : even + 4, R : 2 * R].bitcast(I32)
                 )
+
+        def load_note_scales():
+            stage = tile("xo_stage", [P, 2 * M], U8)
+            for h in range(2):
+                load_scale_pair(stage, xo_scales, h)
+                even = 2 * h * QUADRANT
+                for q in range(2):
+                    first = even + q * QUADRANT
+                    nc.vector.tensor_copy(
+                        xo_s[first : first + 4, :].bitcast(I32),
+                        stage[even : even + 4, q * M : (q + 1) * M].bitcast(I32),
+                    )
 
         def deal(copy, name, src, dtype):
             dealt = tile(name, [P, R], dtype)
@@ -80,10 +97,10 @@ def tile_picked_threebooks_plain_two_boardmeet_one_plain_kernel(
         def fetch(dst, window, lst, scale):
             nc.scalar.activation(dst, window[:].indirect(lst[:]), ACT.Copy, scale=scale)
 
-        xo_s = zeroed("xo_s", M)
-        w_s = zeroed("w_s", R, spare=R)
-        w2_s = zeroed("w2_s", R, spare=R)
-        wb_s = zeroed("wb_s", N)
+        xo_s = scale_tile("xo_s", M)
+        w_s = scale_tile("w_s", R, spare=R)
+        w2_s = scale_tile("w2_s", R, spare=R)
+        wb_s = scale_tile("wb_s", N)
         board = [tile("board" + str(t), [P, C], F32) for t in range(PACK)]
         for t in range(PACK):
             nc.vector.memset(board[t][:], 0.0)
@@ -91,65 +108,60 @@ def tile_picked_threebooks_plain_two_boardmeet_one_plain_kernel(
         xc = tile("xc", [P, J, PACK], BF16)
         xc_codes = tile("xc_codes", [P, J], U32)
         xc_scales = tile("xc_scales", [P, J], U8)
-        got = [[tile("got" + str(pair) + str(i), [P, 2, J], F32) for i in range(3)] for pair in range(2)]
-        two = [tile("two" + str(pair), [P, 2, J], F32) for pair in range(2)]
+        terms = [tile("terms" + str(t), [P, 3, J], F32) for t in range(PACK)]
+        two_terms = [tile("two_terms" + str(t), [P, J], F32) for t in range(PACK)]
 
-        def fetch_pair(pair):
+        def fetch_terms(t):
             for i in range(3):
-                for u in range(2):
-                    t = 2 * pair + u
-                    fetch(got[pair][i][:, u, :], rows[i][t], lists[i], steps[i][:, t : t + 1])
-                if i == 1:
-                    nc.vector.tensor_tensor(two[pair][:], got[pair][0][:], got[pair][1][:], ALU.add)
+                fetch(terms[t][:, i, :], windows[t][i], lists[i], steps[i][:, t : t + 1])
+            nc.vector.tensor_tensor(two_terms[t][:], terms[t][:, 0, :], terms[t][:, 1, :], ALU.add)
 
-        def add_third(pair, slots):
-            nc.vector.tensor_tensor(
-                xc[:, slots, 2 * pair : 2 * pair + 2].rearrange("p (c i) u -> p c u i", i=4),
-                two[pair][:, :, slots].rearrange("p u (c i) -> p c u i", i=4),
-                got[pair][2][:, :, slots].rearrange("p u (c i) -> p c u i", i=4),
-                ALU.add,
-            )
+        def add_third_term(t, slots):
+            nc.vector.tensor_tensor(xc[:, slots, t], two_terms[t][:, slots], terms[t][:, 2, slots], ALU.add)
 
-        load_scale_halves(w_s, w_scales)
-        load_scale_halves(w2_s, w2_scales)
         books = (("ta", ta, offs, ga), ("tb", tb, offs2, gb), ("td", td, offs3, gd))
-        rows, lists, steps = [], [], []
+        windows, lists, steps = [[] for t in range(PACK)], [], []
         for name, table, lst, step in books:
-            rows.append([load_table(name, table, 0)])
+            windows[0].append(load_table(name, table, 0))
             lists.append(load_list(name + "_list", lst))
             steps.append(load_column(name + "_step", step))
-            rows[-1].append(load_table(name, table, 1))
-        load_scale_rows(xo_s, xo_scales, 0)
-        load_scale_rows(xo_s, xo_scales, 2)
-        rows[0].append(load_table("ta", ta, 2))
-        load_scale_rows(xo_s, xo_scales, 1)
-        load_scale_rows(xo_s, xo_scales, 3)
-        rows[0].append(load_table("ta", ta, 3))
+        windows[1].append(load_table("ta", ta, 1))
+        windows[1].append(load_table("tb", tb, 1))
+        load_note_scales()
+        windows[1].append(load_table("td", td, 1))
         note_list = load_list("note_list", offs4)
-        xo_w = load_words("xo_w", xo_words[0], M, U16)
-        for i in (1, 2):
-            for t in (2, 3):
-                rows[i].append(load_table(books[i][0], books[i][1], t))
+        windows[2].append(load_table("ta", ta, 2))
+        load_weight_scales(w_s, w_scales)
+        windows[2].append(load_table("tb", tb, 2))
+        load_weight_scales(w2_s, w2_scales)
+        windows[2].append(load_table("td", td, 2))
+        for name, table, lst, step in books:
+            windows[3].append(load_table(name, table, 3))
         w_w = load_words("w_w", w_words[0], R, U16)
-        put_list = load_list("put_list", offs5)
         w2_w = load_words("w2_w", w2_words[0].rearrange("p c t -> p (c t)"), R, U32)
+        xo_w = load_words("xo_w", xo_words[0], M, U16)
+        put_list = load_list("put_list", offs5)
         slot_list = load_list("slot_list", offs7)
         sb_col = load_column("sb_col", sb)
         place_list = load_list("place_list", offs6)
         sa_col = load_column("sa_col", sa)
         wb_w = load_words("wb_w", wb_words[0].rearrange("p c t -> p (c t)"), N, U32)
         for q in range(4):
-            load_scale_rows(wb_s, wb_scales, q)
+            nc.sync.dma_start(
+                wb_s[QUADRANT * q : QUADRANT * q + 4, :].bitcast(I32), wb_scales[0, 4 * q : 4 * q + 4, :].bitcast(I32)
+            )
 
-        w_sd = deal(nc.vector.tensor_copy, "w_sd", w_s, U8)
-        w2_sd = deal(nc.vector.tensor_copy, "w2_sd", w2_s, U8)
-        fetch_pair(0)
-        add_third(0, slice(0, J))
-        notes_w = tile("notes_w", [P, J], U16)
+        all_slots = slice(0, J)
+        for t in range(2):
+            fetch_terms(t)
+            add_third_term(t, all_slots)
         notes_s = tile("notes_s", [P, J], U8)
         nc.vector.tensor_copy(notes_s[:], xo_s[:].indirect(note_list[:]))
-        nc.vector.tensor_copy(notes_w[:], xo_w[:].indirect(note_list[:]))
-        fetch_pair(1)
+        w_sd = deal(nc.vector.tensor_copy, "w_sd", w_s, U8)
+        w2_sd = deal(nc.vector.tensor_copy, "w2_sd", w2_s, U8)
+        fetch_terms(2)
+        add_third_term(2, all_slots)
+        fetch_terms(3)
         w_wd = deal(nc.scalar.copy, "w_wd", w_w, U16)
         w2_wd = tile("w2_wd", [P, R], U32)
         nc.scalar.copy(w2_wd[:].rearrange("p (t m) -> p m t", t=PACK), w2_w[:].rearrange("p (m t) -> p m t", t=PACK))
@@ -165,7 +177,7 @@ def tile_picked_threebooks_plain_two_boardmeet_one_plain_kernel(
 
         for h in range(2):
             slots = slice(h * HALF, (h + 1) * HALF)
-            add_third(1, slots)
+            add_third_term(PACK - 1, slots)
             nc.vector.quantize_mx(
                 out=xc_codes[:, slots].bitcast(FP8X4), scales=xc_scales[:, slots],
                 in_=xc[:, slots, :].rearrange("p j t -> p (j t)"),
@@ -176,6 +188,9 @@ def tile_picked_threebooks_plain_two_boardmeet_one_plain_kernel(
                     out=a_place(t, h), lhsT=w_wd[:, cols].bitcast(FP4X4), lhsT_scale=w_sd[:, cols],
                     rhs=xc_codes[:, slots].bitcast(FP8X4), rhs_scale=xc_scales[:, slots], start=True, stop=True,
                 )
+
+        notes_w = tile("notes_w", [P, J], U16)
+        nc.vector.tensor_copy(notes_w[:], xo_w[:].indirect(note_list[:]))
 
         a_rows = tile("a_rows", [P, PACK, J], F32)
         nc.scalar.copy(a_rows[:, 0, 0:HALF], banks[0][:, 0:HALF])
@@ -202,27 +217,26 @@ def tile_picked_threebooks_plain_two_boardmeet_one_plain_kernel(
         for h in range(2):
             for t in range(2):
                 nc.vector.tensor_copy(
-                    board[t][:].indirect(put_list[:, h * HALF // 16 : (h + 1) * HALF // 16]),
+                    board[t][:].indirect(put_list[:, h * HALF // LIST_ROWS : (h + 1) * HALF // LIST_ROWS]),
                     a_rows[:, t, h * HALF : (h + 1) * HALF],
                 )
         for t in range(2, PACK):
             nc.vector.tensor_copy(board[t][:].indirect(put_list[:]), a_rows[:, t, :])
 
-        first = tile("first", [P, PACK, O], F32)
+        first_read = tile("first_read", [P, PACK, O], F32)
         for t in range(PACK):
-            fetch(first[:, t, :], board[t], place_list, sa_col[:, t : t + 1])
+            fetch(first_read[:, t, :], board[t], place_list, sa_col[:, t : t + 1])
         diff = tile("diff", [P, PACK, O], F32)
-        nc.vector.tensor_tensor(diff[:, 0:3, :], first[:, 0:3, :], second[:, 0:3, :], ALU.subtract)
-        nc.vector.tensor_tensor(diff[:, 3, :], first[:, 3, :], second[:, 3, :], ALU.subtract)
+        last = PACK - 1
+        nc.vector.tensor_tensor(diff[:, 0:last, :], first_read[:, 0:last, :], second[:, 0:last, :], ALU.subtract)
+        nc.vector.tensor_tensor(diff[:, last, :], first_read[:, last, :], second[:, last, :], ALU.subtract)
 
         hid = tile("hid", [P, O, PACK], BF16)
-        by_place = diff[:].rearrange("p t o -> p o t")
-        nc.vector.scalar_tensor_tensor(
-            hid[:, 0:O_VEC, :], by_place[:, 0:O_VEC, :], -1.0, by_place[:, 0:O_VEC, :], ALU.mult, ALU.max
-        )
+        by_place = diff[:].rearrange("p t o -> p o t")[:, 0:PLACES_ON_VECTOR, :]
+        nc.vector.scalar_tensor_tensor(hid[:, 0:PLACES_ON_VECTOR, :], by_place, -1.0, by_place, ALU.mult, ALU.max)
         nc.scalar.activation(
-            hid[:, O_VEC:O, :].rearrange("p (c i) t -> p c t i", i=4),
-            diff[:, :, O_VEC:O].rearrange("p t (c i) -> p c t i", i=4),
+            hid[:, PLACES_ON_VECTOR:O, :].rearrange("p (c i) t -> p c t i", i=LINE),
+            diff[:, :, PLACES_ON_VECTOR:O].rearrange("p t (c i) -> p c t i", i=LINE),
             ACT.Abs,
         )
         hid_codes = tile("hid_codes", [P, O], U32)
@@ -231,7 +245,7 @@ def tile_picked_threebooks_plain_two_boardmeet_one_plain_kernel(
             out=hid_codes[:].bitcast(FP8X4), scales=hid_scales[:], in_=hid[:].rearrange("p o t -> p (o t)")
         )
 
-        for i in range(2):
+        for i, (copy, queue) in enumerate(((nc.vector.tensor_copy, nc.sync), (nc.scalar.copy, nc.scalar))):
             cols = slice(P * i, P * (i + 1))
             bank = psum.tile([P, O], F32, name="out_bank" + str(i))
             nc.tensor.matmul_mx(
@@ -239,9 +253,5 @@ def tile_picked_threebooks_plain_two_boardmeet_one_plain_kernel(
                 rhs=hid_codes[:].bitcast(FP8X4), rhs_scale=hid_scales[:], start=True, stop=True,
             )
             result = tile("result" + str(i), [P, O], F32)
-            if i == 0:
-                nc.vector.tensor_copy(result[:], bank[:])
-                nc.sync.dma_start(out[cols, :], result[:])
-            else:
-                nc.scalar.copy(result[:], bank[:])
-                nc.scalar.dma_start(out[cols, :], result[:])
+            copy(result[:], bank[:])
+            queue.dma_start(out[cols, :], result[:])

from contextlib import ExitStack

import concourse.mybir as mybir

K, J, R, T, Z, M, O, C, N = 512, 256, 512, 1024, 512, 1024, 128, 512, 256
FLOPS = 2 * (K * R * J + Z * R * J + R * N * O)

F32 = mybir.dt.float32
BF16 = mybir.dt.bfloat16
I32 = mybir.dt.int32
U32 = mybir.dt.uint32
U16 = mybir.dt.uint16
U8 = mybir.dt.uint8
FP8X4 = mybir.dt.float8_e4m3fn_x4
FP4X4 = mybir.dt.float4_e2m1fn_x4
ACT = mybir.ActivationFunctionType
ALU = mybir.AluOpType

P = 128
PACK = 4
QUADRANT = 32
LIST_ROWS = 16
LINE = 4
HALF = J // 2
PLACES_ON_VECTOR = 48


def tile_picked_threebooks_plain_two_boardmeet_one_plain_kernel(
    tc, ta, ga, tb, gb, td, gd, w_words, w_scales, xo_words, xo_scales, w2_words, w2_scales, sa, sb,
    wb_words, wb_scales, offs, offs2, offs3, offs4, offs5, offs6, offs7, out,
):
    nc = tc.nc
    with ExitStack() as ctx:
        keep = ctx.enter_context(tc.tile_pool(name="keep", bufs=1))
        psum = ctx.enter_context(tc.psum_pool(name="psum", bufs=1))

        def tile(name, shape, dtype):
            return keep.tile(shape, dtype, name=name, align_bytes=64)

        def load_list(name, src):
            lst = keep.tile(list(src.shape), U16, name=name)
            nc.sync.dma_start(lst[:], src)
            return lst

        def load_column(name, src):
            col = tile(name, [P, PACK], F32)
            nc.sync.dma_start(col[:], src.rearrange("(p t) o -> p (t o)", t=PACK))
            return col

        def load_table(name, src, t):
            window = tile(name + str(t), [P, T], F32)
            nc.sync.dma_start(window[:], src.rearrange("(p t) c -> p t c", t=PACK)[:, t, :])
            return window

        def load_words(name, src, width, dtype):
            words = tile(name, [P, width], dtype)
            nc.sync.dma_start(words[:].bitcast(I32), src.bitcast(I32))
            return words

        def scale_tile(name, width, spare=0):
            scales = tile(name, [P, width + spare], U8)
            nc.vector.memset(scales[:, 0:width].bitcast(I32), 0)
            return scales

        def load_scale_pair(dst, src, h):
            first = 2 * h * QUADRANT
            nc.sync.dma_start(
                dst[first : first + 4, :].bitcast(I32).rearrange("r (q c) -> r q c", q=2),
                src[0, 8 * h : 8 * h + 8, :].bitcast(I32).rearrange("(q r) c -> r q c", q=2),
            )

        def load_weight_scales(scales, src):
            for h in range(2):
                load_scale_pair(scales, src, h)
                even, odd = 2 * h * QUADRANT, (2 * h + 1) * QUADRANT
                nc.vector.tensor_copy(
                    scales[odd : odd + 4, 0:R].bitcast(I32), scales[even : even + 4, R : 2 * R].bitcast(I32)
                )

        def load_note_scales():
            stage = tile("xo_stage", [P, 2 * M], U8)
            for h in range(2):
                load_scale_pair(stage, xo_scales, h)
                even = 2 * h * QUADRANT
                for q in range(2):
                    first = even + q * QUADRANT
                    nc.vector.tensor_copy(
                        xo_s[first : first + 4, :].bitcast(I32),
                        stage[even : even + 4, q * M : (q + 1) * M].bitcast(I32),
                    )

        def deal(copy, name, src, dtype):
            dealt = tile(name, [P, R], dtype)
            copy(dealt[:].rearrange("p (t m) -> p t m", t=PACK), src[:, 0:R].rearrange("p (m t) -> p t m", t=PACK))
            return dealt

        def fetch(dst, window, lst, scale):
            nc.scalar.activation(dst, window[:].indirect(lst[:]), ACT.Copy, scale=scale)

        xo_s = scale_tile("xo_s", M)
        w_s = scale_tile("w_s", R, spare=R)
        w2_s = scale_tile("w2_s", R, spare=R)
        wb_s = scale_tile("wb_s", N)
        board = [tile("board" + str(t), [P, C], F32) for t in range(PACK)]
        for t in range(PACK):
            nc.vector.memset(board[t][:], 0.0)

        xc = tile("xc", [P, J, PACK], BF16)
        xc_codes = tile("xc_codes", [P, J], U32)
        xc_scales = tile("xc_scales", [P, J], U8)
        terms = [tile("terms" + str(t), [P, 3, J], F32) for t in range(PACK)]
        two_terms = [tile("two_terms" + str(t), [P, J], F32) for t in range(PACK)]

        def fetch_terms(t):
            for i in range(3):
                fetch(terms[t][:, i, :], windows[t][i], lists[i], steps[i][:, t : t + 1])
            nc.vector.tensor_tensor(two_terms[t][:], terms[t][:, 0, :], terms[t][:, 1, :], ALU.add)

        def add_third_term(t, slots):
            nc.vector.tensor_tensor(xc[:, slots, t], two_terms[t][:, slots], terms[t][:, 2, slots], ALU.add)

        books = (("ta", ta, offs, ga), ("tb", tb, offs2, gb), ("td", td, offs3, gd))
        windows, lists, steps = [[] for t in range(PACK)], [], []
        for name, table, lst, step in books:
            windows[0].append(load_table(name, table, 0))
            lists.append(load_list(name + "_list", lst))
            steps.append(load_column(name + "_step", step))
        windows[1].append(load_table("ta", ta, 1))
        windows[1].append(load_table("tb", tb, 1))
        load_note_scales()
        windows[1].append(load_table("td", td, 1))
        note_list = load_list("note_list", offs4)
        windows[2].append(load_table("ta", ta, 2))
        load_weight_scales(w_s, w_scales)
        windows[2].append(load_table("tb", tb, 2))
        load_weight_scales(w2_s, w2_scales)
        windows[2].append(load_table("td", td, 2))
        for name, table, lst, step in books:
            windows[3].append(load_table(name, table, 3))
        w_w = load_words("w_w", w_words[0], R, U16)
        w2_w = load_words("w2_w", w2_words[0].rearrange("p c t -> p (c t)"), R, U32)
        xo_w = load_words("xo_w", xo_words[0], M, U16)
        put_list = load_list("put_list", offs5)
        slot_list = load_list("slot_list", offs7)
        sb_col = load_column("sb_col", sb)
        place_list = load_list("place_list", offs6)
        sa_col = load_column("sa_col", sa)
        wb_w = load_words("wb_w", wb_words[0].rearrange("p c t -> p (c t)"), N, U32)
        for q in range(4):
            nc.sync.dma_start(
                wb_s[QUADRANT * q : QUADRANT * q + 4, :].bitcast(I32), wb_scales[0, 4 * q : 4 * q + 4, :].bitcast(I32)
            )

        all_slots = slice(0, J)
        for t in range(2):
            fetch_terms(t)
            add_third_term(t, all_slots)
        notes_s = tile("notes_s", [P, J], U8)
        nc.vector.tensor_copy(notes_s[:], xo_s[:].indirect(note_list[:]))
        w_sd = deal(nc.vector.tensor_copy, "w_sd", w_s, U8)
        w2_sd = deal(nc.vector.tensor_copy, "w2_sd", w2_s, U8)
        fetch_terms(2)
        add_third_term(2, all_slots)
        fetch_terms(3)
        w_wd = deal(nc.scalar.copy, "w_wd", w_w, U16)
        w2_wd = tile("w2_wd", [P, R], U32)
        nc.scalar.copy(w2_wd[:].rearrange("p (t m) -> p m t", t=PACK), w2_w[:].rearrange("p (m t) -> p m t", t=PACK))

        banks = [psum.tile([P, J], F32, name="bank" + str(i)) for i in range(5)]

        def a_place(t, h):
            if t >= 2:
                return banks[t + 1][:, h * HALF : (h + 1) * HALF]
            if h == 0:
                return banks[t][:, 0:HALF]
            return banks[2][:, t * HALF : (t + 1) * HALF]

        for h in range(2):
            slots = slice(h * HALF, (h + 1) * HALF)
            add_third_term(PACK - 1, slots)
            nc.vector.quantize_mx(
                out=xc_codes[:, slots].bitcast(FP8X4), scales=xc_scales[:, slots],
                in_=xc[:, slots, :].rearrange("p j t -> p (j t)"),
            )
            for t in range(PACK):
                cols = slice(P * t, P * (t + 1))
                nc.tensor.matmul_mx(
                    out=a_place(t, h), lhsT=w_wd[:, cols].bitcast(FP4X4), lhsT_scale=w_sd[:, cols],
                    rhs=xc_codes[:, slots].bitcast(FP8X4), rhs_scale=xc_scales[:, slots], start=True, stop=True,
                )

        notes_w = tile("notes_w", [P, J], U16)
        nc.vector.tensor_copy(notes_w[:], xo_w[:].indirect(note_list[:]))

        a_rows = tile("a_rows", [P, PACK, J], F32)
        nc.scalar.copy(a_rows[:, 0, 0:HALF], banks[0][:, 0:HALF])
        nc.scalar.copy(a_rows[:, 1, 0:HALF], banks[1][:, 0:HALF])
        nc.scalar.copy(a_rows[:, 0:2, HALF:J], banks[2][:].rearrange("p (t j) -> p t j", t=2))
        nc.scalar.copy(a_rows[:, 2, :], banks[3][:])
        nc.scalar.copy(a_rows[:, 3, :], banks[4][:])

        second = tile("second", [P, PACK, O], F32)
        for pair in range(2):
            bank = psum.tile([P, 2, J], F32, name="bank" + str(pair))
            for i in range(2):
                cols = slice(P * (2 * pair + i), P * (2 * pair + i + 1))
                nc.tensor.matmul_mx(
                    out=bank[:, i, :], lhsT=w2_wd[:, cols].bitcast(FP8X4), lhsT_scale=w2_sd[:, cols],
                    rhs=notes_w[:].bitcast(FP4X4), rhs_scale=notes_s[:], start=True, stop=True,
                )
            for i in range(2):
                t = 2 * pair + i
                b_rows = tile("b_rows" + str(t), [P, J], F32)
                nc.scalar.copy(b_rows[:], bank[:, i, :])
                fetch(second[:, t, :], b_rows, slot_list, sb_col[:, t : t + 1])

        for h in range(2):
            for t in range(2):
                nc.vector.tensor_copy(
                    board[t][:].indirect(put_list[:, h * HALF // LIST_ROWS : (h + 1) * HALF // LIST_ROWS]),
                    a_rows[:, t, h * HALF : (h + 1) * HALF],
                )
        for t in range(2, PACK):
            nc.vector.tensor_copy(board[t][:].indirect(put_list[:]), a_rows[:, t, :])

        first_read = tile("first_read", [P, PACK, O], F32)
        for t in range(PACK):
            fetch(first_read[:, t, :], board[t], place_list, sa_col[:, t : t + 1])
        diff = tile("diff", [P, PACK, O], F32)
        last = PACK - 1
        nc.vector.tensor_tensor(diff[:, 0:last, :], first_read[:, 0:last, :], second[:, 0:last, :], ALU.subtract)
        nc.vector.tensor_tensor(diff[:, last, :], first_read[:, last, :], second[:, last, :], ALU.subtract)

        hid = tile("hid", [P, O, PACK], BF16)
        by_place = diff[:].rearrange("p t o -> p o t")[:, 0:PLACES_ON_VECTOR, :]
        nc.vector.scalar_tensor_tensor(hid[:, 0:PLACES_ON_VECTOR, :], by_place, -1.0, by_place, ALU.mult, ALU.max)
        nc.scalar.activation(
            hid[:, PLACES_ON_VECTOR:O, :].rearrange("p (c i) t -> p c t i", i=LINE),
            diff[:, :, PLACES_ON_VECTOR:O].rearrange("p t (c i) -> p c t i", i=LINE),
            ACT.Abs,
        )
        hid_codes = tile("hid_codes", [P, O], U32)
        hid_scales = tile("hid_scales", [P, O], U8)
        nc.vector.quantize_mx(
            out=hid_codes[:].bitcast(FP8X4), scales=hid_scales[:], in_=hid[:].rearrange("p o t -> p (o t)")
        )

        for i, (copy, queue) in enumerate(((nc.vector.tensor_copy, nc.sync), (nc.scalar.copy, nc.scalar))):
            cols = slice(P * i, P * (i + 1))
            bank = psum.tile([P, O], F32, name="out_bank" + str(i))
            nc.tensor.matmul_mx(
                out=bank[:], lhsT=wb_w[:, cols].bitcast(FP8X4), lhsT_scale=wb_s[:, cols],
                rhs=hid_codes[:].bitcast(FP8X4), rhs_scale=hid_scales[:], start=True, stop=True,
            )
            result = tile("result" + str(i), [P, O], F32)
            copy(result[:], bank[:])
            queue.dma_start(out[cols, :], result[:])
